import numpy as np
import ml_dtypes


def mxq(x, axis, fmt="e4m3"):
    dtype, down = {"e4m3": (ml_dtypes.float8_e4m3fn, 7), "e5m2": (ml_dtypes.float8_e5m2, 14)}[fmt]
    v = np.moveaxis(np.asarray(x, np.float32).astype(ml_dtypes.bfloat16).astype(np.float64), axis, -1)
    blocks = v.reshape(v.shape[:-1] + (-1, 32))
    amax = np.abs(blocks).max(-1, keepdims=True)
    byte = np.maximum(np.where(amax > 0, np.frexp(amax)[1] - 1 + 127, 0) - down, 1)
    scale = np.exp2(byte - 127.0)
    codes = (blocks / scale).astype(np.float32).astype(dtype).astype(np.float64)
    return np.moveaxis((codes * scale).reshape(v.shape), -1, axis)


WIDE = False


def mx_kscale(k):
    if not WIDE:
        return np.ones(k)
    levels = np.array([10, -10, 5, -5, 0])
    if k % 512:
        return np.exp2(np.random.permutation(np.resize(levels, k // 32))).repeat(32)
    a = np.empty((k // 512, 16))
    for p in range(k // 512):
        a[p, :8] = np.random.permutation(np.resize(levels, 8))
        for g in range(8):
            far = levels[np.abs(levels - a[p, g]) >= 10]
            a[p, g + 8] = far[np.random.randint(len(far))]
    return np.exp2(a.ravel()).repeat(32)


def f64(x):
    return np.asarray(x).astype(np.float64)


def striped(idx):
    return np.tile(idx.reshape(-1, 16).T, (8, 1)).astype(np.uint16)


def unstriped(offs):
    return offs[:16].T.reshape(-1).astype(np.int64)


def striped8(idx):
    return np.concatenate([x.reshape(-1, 16).T for x in idx]).astype(np.uint16)


def runs(offs, k):
    lists = np.stack([offs[16 * r : 16 * r + 16].T.reshape(-1) for r in range(8)]).astype(np.int64)
    return lists[np.arange(k) % 512 // 64]


def pack_weight(w):
    k, n = w.shape
    w = f64(np.asarray(w, np.float32).astype(ml_dtypes.bfloat16)).reshape(k // 32, 32, n)
    amax = np.abs(w).max(1)
    byte = np.clip(np.where(amax > 0, np.frexp(amax)[1] - 1 + 127 - 7, 1), 1, 254)
    scaled = (w * np.exp2(127.0 - byte)[:, None, :]).reshape(k, n).astype(np.float32)
    words = np.ascontiguousarray(scaled.reshape(k // 512, 128, 4, n).transpose(0, 1, 3, 2)).astype(ml_dtypes.float8_e4m3fn).view(np.uint8)
    return words, np.ascontiguousarray(byte.astype(np.uint8).reshape(k // 512, 16, n))


def unpack_weight(words, scales):
    g, p, n, _ = words.shape
    vals = np.ascontiguousarray(words).view(ml_dtypes.float8_e4m3fn).astype(np.float64) * np.repeat(np.exp2(scales.astype(np.float64) - 127.0), 8, axis=1)[..., None]
    return vals.transpose(0, 1, 3, 2).reshape(g * 512, n)


def sigmoid(v):
    return 1.0 / (1.0 + np.exp(-np.maximum(v, -700.0)))


K, T, S, N, H, G, W = 512, 1024, 512, 512, 512, 2048, 256


def setup_inputs():
    n = np.random.standard_normal
    s = mx_kscale(K)[:, None]
    u = mx_kscale(S)
    packed_xT = pack_weight(n((K, T)) * s)
    packed_dT = pack_weight(n((K, G)) / s)
    perm = np.stack([np.random.permutation(S) for _ in range(8)])
    return {
        "x_words": packed_xT[0],
        "x_scales": packed_xT[1],
        "w1": (n((K, H)) / np.sqrt(K) / s).astype(np.float32),
        "gs": (np.random.uniform(0.5, 1.5, (K, 1)) * s).astype(np.float32),
        "d_words": packed_dT[0],
        "d_scales": packed_dT[1],
        "res": (1.5 * n((N, S))).astype(np.float32),
        "gn": (np.random.uniform(0.5, 1.5, (H, 1)) * u[:, None]).astype(np.float32),
        "w2": (n((H, N)) / np.sqrt(H) / u[:, None]).astype(np.float32),
        "offs": striped(np.random.permutation(T)[:S]),
        "n1": striped8(np.stack([np.random.permutation(S) for _ in range(8)])),
        "n2": striped8(np.stack([np.random.permutation(S) for _ in range(8)])),
        "kidx": striped8(np.random.randint(0, G, (8, H))),
        "n3": striped8(perm[:, :W]),
        "n4": striped8(perm[:, W:]),
    }


def reference(x_words, x_scales, w1, gs, d_words, d_scales, res, gn, w2, offs, n1, n2, kidx, n3, n4):
    d_kidx = unpack_weight(d_words, d_scales)[np.arange(K)[:, None], runs(kidx, K)]
    xq = unpack_weight(x_words, x_scales)[:, unstriped(offs)]
    y = mxq(f64(w1), 0, "e4m3").T @ xq
    z = f64(gs) * (y - (np.minimum(y[np.arange(H)[:, None], runs(n1, H)], y[np.arange(H)[:, None], runs(n2, H)])))
    s = 0.0625 * ((d_kidx.T @ mxq(z, 0, "e4m3")))
    pb = s[np.arange(H)[:, None], runs(n4, H)]
    pa = s[np.arange(H)[:, None], runs(n3, H)]
    rb = pb * sigmoid(pb - pa)
    ra = pa * sigmoid(pa - pb)
    ds = np.zeros((H, S))
    ds[np.arange(H)[:, None], runs(n3, H)] = ra
    dt = ds.copy()
    dt[np.arange(H)[:, None], runs(n4, H)] = rb
    z2 = f64(gn) * dt
    return f64(res) + (mxq(f64(w2), 0, "e4m3").T @ mxq(z2, 0, "e4m3"))

@@ -1,0 +1,246 @@
+from contextlib import ExitStack
+
+import concourse.mybir as mybir
+
+K, T, S, N, H, G, W = 512, 1024, 512, 512, 512, 2048, 256
+FLOPS = 3 * 2 * 512 * 512 * 512
+
+F32 = mybir.dt.float32
+BF16 = mybir.dt.bfloat16
+U32 = mybir.dt.uint32
+I32 = mybir.dt.int32
+U16 = mybir.dt.uint16
+U8 = mybir.dt.uint8
+FP8X4 = mybir.dt.float8_e4m3fn_x4
+ALU = mybir.AluOpType
+ACT = mybir.ActivationFunctionType
+
+P = 128
+PACK = 4
+HALF = 256
+TAIL = 128
+
+
+def tile_picked_pqkunderduel_none_p_kernel(
+    tc, x_words, x_scales, w1, gs, d_words, d_scales, res, gn, w2, offs, n1, n2, kidx, n3, n4, out
+):
+    nc = tc.nc
+    with ExitStack() as ctx:
+        lists = ctx.enter_context(tc.tile_pool(name="lists", bufs=1))
+        keep = ctx.enter_context(tc.tile_pool(name="keep", bufs=1))
+        ring = ctx.enter_context(tc.tile_pool(name="ring", bufs=3))
+        psum = ctx.enter_context(tc.psum_pool(name="psum", bufs=1))
+
+        def load_list(src, name):
+            dst = lists.tile(list(src.shape), U16, name=name)
+            nc.sync.dma_start(dst[:], src)
+            return dst
+
+        def kt(shape, dtype, name, tag=None):
+            return keep.tile(shape, dtype, name=name, tag=tag or name, align_bytes=64)
+
+        xs_tab = kt([P, T], U8, "xs_tab")
+        ds_tab = kt([P, G], U8, "ds_tab")
+        ds_fin = kt([P, H], U8, "ds_fin")
+        nc.vector.memset(xs_tab[:].bitcast(I32), 0)
+        nc.vector.memset(ds_tab[:].bitcast(I32), 0)
+        nc.gpsimd.memset(ds_fin[:].bitcast(I32), 0)
+        warm = kt([P, 2], F32, "warm")
+        nc.gpsimd.memset(warm[:, 0:1], 0.0)
+        nc.scalar.activation(warm[:, 1:2], warm[:, 0:1], ACT.Sigmoid)
+
+        offs_t = load_list(offs, "offs_t")
+        xw_tab = kt([P, T], U32, "xw_tab")
+        nc.sync.dma_start(xw_tab[:].bitcast(I32), x_words[0].rearrange("p c r -> p (c r)").bitcast(I32))
+        for q in range(4):
+            nc.scalar.dma_start(xs_tab[32 * q : 32 * q + 4, :].bitcast(I32), x_scales[0, 4 * q : 4 * q + 4, :].bitcast(I32))
+        w1_rows = w1.rearrange("(p j) c -> p j c", j=PACK)
+        w1_raw = []
+        for h in range(2):
+            raw = kt([P, PACK, HALF], F32, f"w1_raw{h}")
+            nc.sync.dma_start(raw[:], w1_rows[:, :, h * HALF : (h + 1) * HALF])
+            w1_raw.append(raw)
+        kidx_t = load_list(kidx, "kidx_t")
+        for q in range(4):
+            nc.sync.dma_start(ds_tab[32 * q + 14 : 32 * q + 18, :].bitcast(I32), d_scales[0, 4 * q : 4 * q + 4, :].bitcast(I32))
+        n1_t = load_list(n1, "n1_t")
+        n2_t = load_list(n2, "n2_t")
+        gs_t = kt([P, PACK], F32, "gs_t")
+        nc.sync.dma_start(gs_t[:], gs.rearrange("(p t) o -> p (t o)", t=PACK))
+        w2_raw = kt([P, PACK, N], F32, "w2_raw")
+        nc.sync.dma_start(w2_raw[:], w2.rearrange("(p j) c -> p j c", j=PACK))
+        dw_tab = kt([P, G], U32, "dw_tab")
+        nc.sync.dma_start(dw_tab[:].bitcast(I32), d_words[0].rearrange("p c r -> p (c r)").bitcast(I32))
+        n3_t = load_list(n3, "n3_t")
+        n4_t = load_list(n4, "n4_t")
+        gn_t = kt([P, PACK], F32, "gn_t")
+        nc.sync.dma_start(gn_t[:], gn.rearrange("(p t) o -> p (t o)", t=PACK))
+        res_t = kt([P, PACK, S], F32, "res_t")
+        nc.sync.dma_start(res_t[:], res.rearrange("(t p) j -> p t j", p=P))
+
+        xs = kt([P, S], U8, "xs")
+        nc.vector.tensor_copy(xs[:], xs_tab[:].indirect(offs_t[:]))
+        xw = kt([P, S], U32, "xw")
+        nc.vector.tensor_copy(xw[:], xw_tab[:].indirect(offs_t[:]))
+
+        w1_bf = kt([P, PACK, P, PACK], BF16, "w1_bf")
+
+        def w1_views(h, c0, c1):
+            m0, m1 = (h * HALF + c0) // PACK, (h * HALF + c1) // PACK
+            dst = w1_bf[:, :, m0:m1, :].rearrange("p t m j -> p m j t")
+            src = w1_raw[h][:, :, c0:c1].rearrange("p j (m t) -> p m j t", t=PACK)
+            return dst, src
+
+        nc.scalar.copy(*w1_views(0, 0, HALF))
+        ds_g = kt([P, H], U8, "ds_g")
+        nc.vector.tensor_copy(ds_g[:], ds_tab[:].indirect(kidx_t[:]))
+        nc.scalar.copy(*w1_views(1, 0, HALF // 2))
+        nc.vector.tensor_copy(*w1_views(1, HALF // 2, HALF))
+
+        w1_c = kt([P, H], U32, "w1_c")
+        w1_s = kt([P, H], U8, "w1_s")
+        y = []
+        for t in range(PACK):
+            cols = slice(t * P, (t + 1) * P)
+            nc.vector.quantize_mx(w1_c[:, cols].bitcast(FP8X4), w1_s[:, cols], w1_bf[:, t].rearrange("p m j -> p (m j)"))
+            acc = psum.tile([P, S], F32, name=f"acc_y{t}", tag=f"bank{t}")
+            nc.tensor.matmul_mx(acc[:], lhsT=w1_c[:, cols].bitcast(FP8X4), lhsT_scale=w1_s[:, cols],
+                                rhs=xw[:].bitcast(FP8X4), rhs_scale=xs[:], start=True, stop=True)
+            y_t = kt([P, S], F32, f"y{t}")
+            nc.scalar.copy(y_t[:], acc[:])
+            y.append(y_t)
+
+        ds_d = kt([P, H], U8, "ds_d")
+        nc.vector.tensor_copy(ds_d[:].rearrange("p (t m) -> p m t", t=PACK), ds_g[:].rearrange("p (m t) -> p m t", t=PACK))
+        for q in range(4):
+            nc.sync.dma_start(ds_fin[32 * q : 32 * q + 4, :].bitcast(I32), ds_d[32 * q + 14 : 32 * q + 18, :].bitcast(I32))
+
+        z_bf = [kt([P, HALF, PACK], BF16, f"z_bf{h}", tag=f"z_bf{h}") for h in range(2)]
+        w2_bf = kt([P, N, PACK], BF16, "w2_bf")
+        steps = [(t, h) for t in range(PACK) for h in range(2)]
+        picked, least = {}, {}
+
+        def fetch(i, which):
+            t, h = steps[i]
+            if which == 0:
+                picked[i] = ring.tile([P, 2, HALF], F32, name="picked")
+            lst = (n1_t, n2_t)[which]
+            nc.vector.tensor_copy(picked[i][:, which, :], y[t][:].indirect(lst[:, h * 16 : (h + 1) * 16]))
+
+        def smaller(i):
+            if i == len(steps) - 1:
+                least[i] = kt([P, HALF], F32, "least_last", tag="hold_d")
+            else:
+                least[i] = ring.tile([P, HALF], F32, name="least")
+            nc.vector.tensor_tensor(least[i][:], picked[i][:, 0, :], picked[i][:, 1, :], ALU.min)
+
+        def above(i):
+            t, h = steps[i]
+            gap = ring.tile([P, HALF], F32, name="gap")
+            nc.vector.tensor_tensor(gap[:], y[t][:, h * HALF : (h + 1) * HALF], least[i][:], ALU.subtract)
+            nc.scalar.activation(z_bf[h][:, :, t], gap[:], ACT.Copy, scale=gs_t[:, t : t + 1])
+
+        def cast_w2(c):
+            cols = slice(c * P, (c + 1) * P)
+            nc.scalar.copy(w2_bf[:, cols, :].rearrange("p (c i) j -> p c j i", i=4),
+                           w2_raw[:, :, cols].rearrange("p j (c i) -> p c j i", i=4))
+
+        z_c = kt([P, S], U32, "z_c")
+        z_s = kt([P, S], U8, "z_s")
+
+        def quant_z(h):
+            cols = slice(h * HALF, (h + 1) * HALF)
+            nc.vector.quantize_mx(z_c[:, cols].bitcast(FP8X4), z_s[:, cols], z_bf[h][:].rearrange("p c t -> p (c t)"))
+
+        for i in range(len(steps) + 1):
+            if i < len(steps):
+                fetch(i, 0)
+            if i >= 1:
+                smaller(i - 1)
+            if i < len(steps):
+                fetch(i, 1)
+            if i >= 1:
+                above(i - 1)
+            if 2 <= i < 6:
+                cast_w2(i - 2)
+
+        dw_g = kt([P, H], U32, "dw_g", tag="hold_d")
+        nc.vector.tensor_copy(dw_g[:], dw_tab[:].indirect(kidx_t[:]))
+        quant_z(0)
+        dw_d = kt([P, H], U32, "dw_d")
+        nc.vector.tensor_copy(dw_d[:].rearrange("p (t m) -> p m t", t=PACK), dw_g[:].rearrange("p (m t) -> p m t", t=PACK))
+        quant_z(1)
+        w2_c = kt([P, N], U32, "w2_c", tag="z_bf1")
+        w2_s = kt([P, N], U8, "w2_s")
+        nc.vector.quantize_mx(w2_c[:].bitcast(FP8X4), w2_s[:], w2_bf[:].rearrange("p c j -> p (c j)"))
+
+        s = [kt([P, S], F32, f"s{t}") for t in range(PACK)]
+        for t in range(PACK):
+            keys = slice(t * P, (t + 1) * P)
+            for h in range(2):
+                cols = slice(h * HALF, (h + 1) * HALF)
+                acc = psum.tile([P, HALF], F32, name=f"acc_s{t}{h}", tag=f"bank{4 * (1 - h) + t}")
+                nc.tensor.matmul_mx(acc[:], lhsT=dw_d[:, keys].bitcast(FP8X4), lhsT_scale=ds_fin[:, keys],
+                                    rhs=z_c[:, cols].bitcast(FP8X4), rhs_scale=z_s[:, cols], start=True, stop=True)
+                nc.scalar.activation(s[t][:, cols], acc[:], ACT.Copy, scale=0.0625)
+
+        z2_bf = [kt([P, TAIL, PACK], BF16, f"z2_bf{c}") for c in range(S // TAIL)]
+        pair = [kt([P, 2, W], F32, f"pair{t}") for t in range(PACK)]
+        odds = [kt([P, 2, W], F32, f"odds{t}") for t in range(PACK)]
+        dt = [kt([P, S], F32, f"dt{t}") for t in range(PACK)]
+
+        def fetch_pair(t, which):
+            nc.vector.tensor_copy(pair[t][:, which, :], s[t][:].indirect((n3_t, n4_t)[which][:]))
+
+        def lead(t):
+            diff = ring.tile([P, W], F32, name="diff")
+            nc.vector.tensor_tensor(diff[:], pair[t][:, 0, :], pair[t][:, 1, :], ALU.subtract)
+            nc.scalar.activation(odds[t][:, 0, :], diff[:], ACT.Sigmoid)
+            nc.scalar.activation(odds[t][:, 1, :], diff[:], ACT.Sigmoid, scale=-1.0)
+
+        def put(t, which):
+            nc.vector.tensor_tensor(dt[t][:].indirect((n3_t, n4_t)[which][:]), pair[t][:, which, :], odds[t][:, which, :], ALU.mult)
+
+        def cast_z2(t):
+            for c in range(S // TAIL):
+                nc.scalar.activation(z2_bf[c][:, :, t], dt[t][:, c * TAIL : (c + 1) * TAIL], ACT.Copy, scale=gn_t[:, t : t + 1])
+
+        for t in range(PACK + 1):
+            if t < PACK:
+                fetch_pair(t, 0)
+            if t >= 1:
+                lead(t - 1)
+            if t < PACK:
+                fetch_pair(t, 1)
+        put(0, 0)
+        for t in range(PACK):
+            if t + 1 < PACK:
+                put(t + 1, 0)
+            put(t, 1)
+            cast_z2(t)
+
+        z2_c = kt([P, S], U32, "z2_c")
+        z2_s = kt([P, S], U8, "z2_s")
+        out_rows = out.rearrange("(t p) j -> p t j", p=P)
+        accs = {}
+
+        def product(c):
+            cols = slice(c * TAIL, (c + 1) * TAIL)
+            nc.vector.quantize_mx(z2_c[:, cols].bitcast(FP8X4), z2_s[:, cols], z2_bf[c][:].rearrange("p c t -> p (c t)"))
+            accs[c] = psum.tile([P, PACK, TAIL], F32, name=f"acc_o{c}", tag=f"bank{c}")
+            for t in range(PACK):
+                rows = slice(t * P, (t + 1) * P)
+                nc.tensor.matmul_mx(accs[c][:, t, :], lhsT=w2_c[:, rows].bitcast(FP8X4), lhsT_scale=w2_s[:, rows],
+                                    rhs=z2_c[:, cols].bitcast(FP8X4), rhs_scale=z2_s[:, cols], start=True, stop=True)
+
+        def finish(c):
+            cols = slice(c * TAIL, (c + 1) * TAIL)
+            total = kt([P, PACK, TAIL], F32, f"total{c}")
+            nc.vector.tensor_tensor(total[:], accs[c][:], res_t[:, :, cols], ALU.add)
+            nc.sync.dma_start(out_rows[:, :, cols], total[:])
+
+        for c in range(S // TAIL + 1):
+            if c < S // TAIL:
+                product(c)
+            if c >= 1:
+                finish(c - 1)

@@ -117,28 +117,33 @@ def tile_picked_pqkunderduel_none_p_kernel(
 
         z_bf = [kt([P, HALF, PACK], BF16, f"z_bf{h}", tag=f"z_bf{h}") for h in range(2)]
         w2_bf = kt([P, N, PACK], BF16, "w2_bf")
-        steps = [(t, h) for t in range(PACK) for h in range(2)]
+        steps = [(t, 0, S) for t in range(PACK - 1)] + [(PACK - 1, 0, HALF), (PACK - 1, HALF, S)]
+        last = len(steps) - 1
         picked, least = {}, {}
 
-        def fetch(i, which):
-            t, h = steps[i]
-            if which == 0:
-                picked[i] = ring.tile([P, 2, HALF], F32, name="picked")
+        def fetch(i, k):
+            t, c0, c1 = steps[i]
+            if k == 0:
+                if i == last - 1:
+                    picked[i] = kt([P, 2, c1 - c0], F32, "picked_late", tag="hold_w2")
+                else:
+                    picked[i] = ring.tile([P, 2, c1 - c0], F32, name="picked")
+            which, off = k % 2, (k // 2) * HALF
             lst = (n1_t, n2_t)[which]
-            nc.vector.tensor_copy(picked[i][:, which, :], y[t][:].indirect(lst[:, h * 16 : (h + 1) * 16]))
+            nc.vector.tensor_copy(picked[i][:, which, off : off + HALF],
+                                  y[t][:].indirect(lst[:, (c0 + off) // 16 : (c0 + off + HALF) // 16]))
 
         def smaller(i):
-            if i == len(steps) - 1:
-                least[i] = kt([P, HALF], F32, "least_last", tag="hold_d")
+            t, c0, c1 = steps[i]
+            if i == last:
+                least = kt([P, c1 - c0], F32, "least_last", tag="hold_d")
             else:
-                least[i] = ring.tile([P, HALF], F32, name="least")
-            nc.vector.tensor_tensor(least[i][:], picked[i][:, 0, :], picked[i][:, 1, :], ALU.min)
-
-        def above(i):
-            t, h = steps[i]
-            gap = ring.tile([P, HALF], F32, name="gap")
-            nc.vector.tensor_tensor(gap[:], y[t][:, h * HALF : (h + 1) * HALF], least[i][:], ALU.subtract)
-            nc.scalar.activation(z_bf[h][:, :, t], gap[:], ACT.Copy, scale=gs_t[:, t : t + 1])
+                least = ring.tile([P, c1 - c0], F32, name="least")
+            nc.vector.tensor_tensor(least[:], picked[i][:, 0, :], picked[i][:, 1, :], ALU.min)
+            gap = ring.tile([P, c1 - c0], F32, name="gap")
+            nc.gpsimd.tensor_tensor(gap[:], y[t][:, c0:c1], least[:], ALU.subtract)
+            for c in range(c0, c1, HALF):
+                nc.scalar.activation(z_bf[c // HALF][:, :, t], gap[:, c - c0 : c - c0 + HALF], ACT.Copy, scale=gs_t[:, t : t + 1])
 
         def cast_w2(c):
             cols = slice(c * P, (c + 1) * P)
@@ -147,22 +152,30 @@ def tile_picked_pqkunderduel_none_p_kernel(
 
         z_c = kt([P, S], U32, "z_c")
         z_s = kt([P, S], U8, "z_s")
+        w2_c, w2_s = {}, {}
 
         def quant_z(h):
             cols = slice(h * HALF, (h + 1) * HALF)
             nc.vector.quantize_mx(z_c[:, cols].bitcast(FP8X4), z_s[:, cols], z_bf[h][:].rearrange("p c t -> p (c t)"))
 
-        for i in range(len(steps) + 1):
-            if i < len(steps):
-                fetch(i, 0)
+        def quant_w2(h):
+            w2_c[h] = kt([P, HALF], U32, f"w2_c{h}", tag=("hold_w2", "z_bf1")[h])
+            w2_s[h] = kt([P, HALF], U8, f"w2_s{h}")
+            nc.vector.quantize_mx(w2_c[h][:].bitcast(FP8X4), w2_s[h][:],
+                                  w2_bf[:, h * HALF : (h + 1) * HALF, :].rearrange("p c j -> p (c j)"))
+
+        for i in range(last + 1):
+            t, c0, c1 = steps[i]
+            fetch(i, 0)
             if i >= 1:
                 smaller(i - 1)
-            if i < len(steps):
-                fetch(i, 1)
-            if i >= 1:
-                above(i - 1)
-            if 2 <= i < 6:
-                cast_w2(i - 2)
+            for k in range(1, 2 * (c1 - c0) // HALF):
+                fetch(i, k)
+            if i < 2:
+                cast_w2(2 * i)
+                cast_w2(2 * i + 1)
+        quant_w2(0)
+        smaller(last)
 
         dw_g = kt([P, H], U32, "dw_g", tag="hold_d")
         nc.vector.tensor_copy(dw_g[:], dw_tab[:].indirect(kidx_t[:]))
@@ -170,9 +183,7 @@ def tile_picked_pqkunderduel_none_p_kernel(
         dw_d = kt([P, H], U32, "dw_d")
         nc.vector.tensor_copy(dw_d[:].rearrange("p (t m) -> p m t", t=PACK), dw_g[:].rearrange("p (m t) -> p m t", t=PACK))
         quant_z(1)
-        w2_c = kt([P, N], U32, "w2_c", tag="z_bf1")
-        w2_s = kt([P, N], U8, "w2_s")
-        nc.vector.quantize_mx(w2_c[:].bitcast(FP8X4), w2_s[:], w2_bf[:].rearrange("p c j -> p (c j)"))
+        quant_w2(1)
 
         s = [kt([P, S], F32, f"s{t}") for t in range(PACK)]
         for t in range(PACK):
@@ -194,7 +205,8 @@ def tile_picked_pqkunderduel_none_p_kernel(
 
         def lead(t):
             diff = ring.tile([P, W], F32, name="diff")
-            nc.vector.tensor_tensor(diff[:], pair[t][:, 0, :], pair[t][:, 1, :], ALU.subtract)
+            eng = nc.vector if t == PACK - 1 else nc.gpsimd
+            eng.tensor_tensor(diff[:], pair[t][:, 0, :], pair[t][:, 1, :], ALU.subtract)
             nc.scalar.activation(odds[t][:, 0, :], diff[:], ACT.Sigmoid)
             nc.scalar.activation(odds[t][:, 1, :], diff[:], ACT.Sigmoid, scale=-1.0)
 
@@ -205,14 +217,13 @@ def tile_picked_pqkunderduel_none_p_kernel(
             for c in range(S // TAIL):
                 nc.scalar.activation(z2_bf[c][:, :, t], dt[t][:, c * TAIL : (c + 1) * TAIL], ACT.Copy, scale=gn_t[:, t : t + 1])
 
-        for t in range(PACK + 1):
-            if t < PACK:
-                fetch_pair(t, 0)
-            if t >= 1:
-                lead(t - 1)
-            if t < PACK:
-                fetch_pair(t, 1)
+        for t in range(PACK):
+            fetch_pair(t, 0)
+            fetch_pair(t, 1)
+            if t < PACK - 1:
+                lead(t)
         put(0, 0)
+        lead(PACK - 1)
         for t in range(PACK):
             if t + 1 < PACK:
                 put(t + 1, 0)
@@ -229,8 +240,8 @@ def tile_picked_pqkunderduel_none_p_kernel(
             nc.vector.quantize_mx(z2_c[:, cols].bitcast(FP8X4), z2_s[:, cols], z2_bf[c][:].rearrange("p c t -> p (c t)"))
             accs[c] = psum.tile([P, PACK, TAIL], F32, name=f"acc_o{c}", tag=f"bank{c}")
             for t in range(PACK):
-                rows = slice(t * P, (t + 1) * P)
-                nc.tensor.matmul_mx(accs[c][:, t, :], lhsT=w2_c[:, rows].bitcast(FP8X4), lhsT_scale=w2_s[:, rows],
+                rows = slice(t % 2 * P, (t % 2 + 1) * P)
+                nc.tensor.matmul_mx(accs[c][:, t, :], lhsT=w2_c[t // 2][:, rows].bitcast(FP8X4), lhsT_scale=w2_s[t // 2][:, rows],
                                     rhs=z2_c[:, cols].bitcast(FP8X4), rhs_scale=z2_s[:, cols], start=True, stop=True)
 
         def finish(c):

@@ -42,23 +42,23 @@ def tile_picked_pqkunderduel_none_p_kernel(
         xs_tab = kt([P, T], U8, "xs_tab")
         ds_tab = kt([P, G], U8, "ds_tab")
         ds_fin = kt([P, H], U8, "ds_fin")
-        nc.vector.memset(xs_tab[:].bitcast(I32), 0)
-        nc.vector.memset(ds_tab[:].bitcast(I32), 0)
-        nc.gpsimd.memset(ds_fin[:].bitcast(I32), 0)
         warm = kt([P, 2], F32, "warm")
+        nc.gpsimd.memset(xs_tab[:].bitcast(I32), 0)
         nc.gpsimd.memset(warm[:, 0:1], 0.0)
-        nc.scalar.activation(warm[:, 1:2], warm[:, 0:1], ACT.Sigmoid)
+        nc.gpsimd.memset(ds_tab[:].bitcast(I32), 0)
+        nc.gpsimd.memset(ds_fin[:].bitcast(I32), 0)
 
         offs_t = load_list(offs, "offs_t")
-        xw_tab = kt([P, T], U32, "xw_tab")
-        nc.sync.dma_start(xw_tab[:].bitcast(I32), x_words[0].rearrange("p c r -> p (c r)").bitcast(I32))
         for q in range(4):
             nc.scalar.dma_start(xs_tab[32 * q : 32 * q + 4, :].bitcast(I32), x_scales[0, 4 * q : 4 * q + 4, :].bitcast(I32))
+        nc.scalar.activation(warm[:, 1:2], warm[:, 0:1], ACT.Sigmoid)
+        xw_tab = kt([P, T], U32, "xw_tab")
+        nc.sync.dma_start(xw_tab[:].bitcast(I32), x_words[0].rearrange("p c r -> p (c r)").bitcast(I32))
         w1_rows = w1.rearrange("(p j) c -> p j c", j=PACK)
         w1_raw = []
-        for h in range(2):
-            raw = kt([P, PACK, HALF], F32, f"w1_raw{h}")
-            nc.sync.dma_start(raw[:], w1_rows[:, :, h * HALF : (h + 1) * HALF])
+        for u in range(2):
+            raw = kt([P, 2, H], F32, f"w1_raw{u}", tag=f"w1_raw{u}")
+            nc.sync.dma_start(raw[:], w1_rows[:, 2 * u : 2 * u + 2, :])
             w1_raw.append(raw)
         kidx_t = load_list(kidx, "kidx_t")
         for q in range(4):
@@ -67,14 +67,16 @@ def tile_picked_pqkunderduel_none_p_kernel(
         n2_t = load_list(n2, "n2_t")
         gs_t = kt([P, PACK], F32, "gs_t")
         nc.sync.dma_start(gs_t[:], gs.rearrange("(p t) o -> p (t o)", t=PACK))
-        w2_raw = kt([P, PACK, N], F32, "w2_raw")
-        nc.sync.dma_start(w2_raw[:], w2.rearrange("(p j) c -> p j c", j=PACK))
+        gs_neg = kt([P, PACK], F32, "gs_neg")
+        nc.scalar.mul(gs_neg[:], gs_t[:], -1.0)
         dw_tab = kt([P, G], U32, "dw_tab")
         nc.sync.dma_start(dw_tab[:].bitcast(I32), d_words[0].rearrange("p c r -> p (c r)").bitcast(I32))
         n3_t = load_list(n3, "n3_t")
         n4_t = load_list(n4, "n4_t")
         gn_t = kt([P, PACK], F32, "gn_t")
         nc.sync.dma_start(gn_t[:], gn.rearrange("(p t) o -> p (t o)", t=PACK))
+        w2_raw = kt([P, PACK, N], F32, "w2_raw")
+        nc.sync.dma_start(w2_raw[:], w2.rearrange("(p j) c -> p j c", j=PACK))
         res_t = kt([P, PACK, S], F32, "res_t")
         nc.sync.dma_start(res_t[:], res.rearrange("(t p) j -> p t j", p=P))
 
@@ -83,86 +85,69 @@ def tile_picked_pqkunderduel_none_p_kernel(
         xw = kt([P, S], U32, "xw")
         nc.vector.tensor_copy(xw[:], xw_tab[:].indirect(offs_t[:]))
 
-        w1_bf = kt([P, PACK, P, PACK], BF16, "w1_bf")
-
-        def w1_views(h, c0, c1):
-            m0, m1 = (h * HALF + c0) // PACK, (h * HALF + c1) // PACK
-            dst = w1_bf[:, :, m0:m1, :].rearrange("p t m j -> p m j t")
-            src = w1_raw[h][:, :, c0:c1].rearrange("p j (m t) -> p m j t", t=PACK)
-            return dst, src
-
-        nc.scalar.copy(*w1_views(0, 0, HALF))
-        ds_g = kt([P, H], U8, "ds_g")
-        nc.vector.tensor_copy(ds_g[:], ds_tab[:].indirect(kidx_t[:]))
-        nc.scalar.copy(*w1_views(1, 0, HALF // 2))
-        nc.vector.tensor_copy(*w1_views(1, HALF // 2, HALF))
+        w1_bf = [kt([P, 2, P, PACK], BF16, f"w1_bf{v}") for v in range(2)]
+        for u in range(2):
+            for v in range(2):
+                copy = nc.vector.tensor_copy if (u, v) == (1, 0) else nc.scalar.copy
+                dst = w1_bf[v][:, :, :, 2 * u : 2 * u + 2].rearrange("p t m j -> p m j t")
+                src = w1_raw[u][:].rearrange("p j (m t) -> p m j t", t=PACK)[:, :, :, 2 * v : 2 * v + 2]
+                copy(dst, src)
 
         w1_c = kt([P, H], U32, "w1_c")
         w1_s = kt([P, H], U8, "w1_s")
-        y = []
+        y, y_again = [], []
         for t in range(PACK):
             cols = slice(t * P, (t + 1) * P)
-            nc.vector.quantize_mx(w1_c[:, cols].bitcast(FP8X4), w1_s[:, cols], w1_bf[:, t].rearrange("p m j -> p (m j)"))
+            nc.vector.quantize_mx(w1_c[:, cols].bitcast(FP8X4), w1_s[:, cols], w1_bf[t // 2][:, t % 2].rearrange("p m j -> p (m j)"))
             acc = psum.tile([P, S], F32, name=f"acc_y{t}", tag=f"bank{t}")
             nc.tensor.matmul_mx(acc[:], lhsT=w1_c[:, cols].bitcast(FP8X4), lhsT_scale=w1_s[:, cols],
                                 rhs=xw[:].bitcast(FP8X4), rhs_scale=xs[:], start=True, stop=True)
             y_t = kt([P, S], F32, f"y{t}")
+            twin = kt([P, S], F32, f"y_again{t}")
+            nc.scalar.copy(twin[:, :HALF], acc[:, :HALF])
             nc.scalar.copy(y_t[:], acc[:])
+            nc.scalar.copy(twin[:, HALF:], acc[:, HALF:])
             y.append(y_t)
+            y_again.append(twin)
 
+        ds_g = kt([P, H], U8, "ds_g", tag="w1_raw1")
+        nc.vector.tensor_copy(ds_g[:], ds_tab[:].indirect(kidx_t[:]))
         ds_d = kt([P, H], U8, "ds_d")
         nc.vector.tensor_copy(ds_d[:].rearrange("p (t m) -> p m t", t=PACK), ds_g[:].rearrange("p (m t) -> p m t", t=PACK))
         for q in range(4):
             nc.sync.dma_start(ds_fin[32 * q : 32 * q + 4, :].bitcast(I32), ds_d[32 * q + 14 : 32 * q + 18, :].bitcast(I32))
 
         z_bf = [kt([P, HALF, PACK], BF16, f"z_bf{h}", tag=f"z_bf{h}") for h in range(2)]
-        w2_bf = kt([P, N, PACK], BF16, "w2_bf")
         steps = [(t, 0, S) for t in range(PACK - 1)] + [(PACK - 1, 0, HALF), (PACK - 1, HALF, S)]
         last = len(steps) - 1
-        picked, least = {}, {}
+        picked = {}
 
         def fetch(i, k):
             t, c0, c1 = steps[i]
             if k == 0:
                 if i == last - 1:
-                    picked[i] = kt([P, 2, c1 - c0], F32, "picked_late", tag="hold_w2")
+                    picked[i] = kt([P, 2, c1 - c0], F32, "picked_late", tag="hold_d")
                 else:
                     picked[i] = ring.tile([P, 2, c1 - c0], F32, name="picked")
             which, off = k % 2, (k // 2) * HALF
             lst = (n1_t, n2_t)[which]
-            nc.vector.tensor_copy(picked[i][:, which, off : off + HALF],
-                                  y[t][:].indirect(lst[:, (c0 + off) // 16 : (c0 + off + HALF) // 16]))
+            nc.vector.tensor_tensor(picked[i][:, which, off : off + HALF],
+                                    y[t][:].indirect(lst[:, (c0 + off) // 16 : (c0 + off + HALF) // 16]),
+                                    y_again[t][:, c0 + off : c0 + off + HALF], ALU.subtract)
 
         def smaller(i):
             t, c0, c1 = steps[i]
-            if i == last:
-                least = kt([P, c1 - c0], F32, "least_last", tag="hold_d")
-            else:
-                least = ring.tile([P, c1 - c0], F32, name="least")
+            least = ring.tile([P, c1 - c0], F32, name="least")
             nc.vector.tensor_tensor(least[:], picked[i][:, 0, :], picked[i][:, 1, :], ALU.min)
-            gap = ring.tile([P, c1 - c0], F32, name="gap")
-            nc.gpsimd.tensor_tensor(gap[:], y[t][:, c0:c1], least[:], ALU.subtract)
             for c in range(c0, c1, HALF):
-                nc.scalar.activation(z_bf[c // HALF][:, :, t], gap[:, c - c0 : c - c0 + HALF], ACT.Copy, scale=gs_t[:, t : t + 1])
-
-        def cast_w2(c):
-            cols = slice(c * P, (c + 1) * P)
-            nc.scalar.copy(w2_bf[:, cols, :].rearrange("p (c i) j -> p c j i", i=4),
-                           w2_raw[:, :, cols].rearrange("p j (c i) -> p c j i", i=4))
+                nc.scalar.activation(z_bf[c // HALF][:, :, t], least[:, c - c0 : c - c0 + HALF], ACT.Copy, scale=gs_neg[:, t : t + 1])
 
         z_c = kt([P, S], U32, "z_c")
         z_s = kt([P, S], U8, "z_s")
-        w2_c, w2_s = {}, {}
 
         def quant_z(h):
             cols = slice(h * HALF, (h + 1) * HALF)
             nc.vector.quantize_mx(z_c[:, cols].bitcast(FP8X4), z_s[:, cols], z_bf[h][:].rearrange("p c t -> p (c t)"))
-
-        def quant_w2(h):
-            w2_c[h] = kt([P, HALF], U32, f"w2_c{h}", tag=("hold_w2", "z_bf1")[h])
-            w2_s[h] = kt([P, HALF], U8, f"w2_s{h}")
-            nc.vector.quantize_mx(w2_c[h][:].bitcast(FP8X4), w2_s[h][:],
-                                  w2_bf[:, h * HALF : (h + 1) * HALF, :].rearrange("p c j -> p (c j)"))
 
         for i in range(last + 1):
             t, c0, c1 = steps[i]
@@ -171,19 +156,18 @@ def tile_picked_pqkunderduel_none_p_kernel(
                 smaller(i - 1)
             for k in range(1, 2 * (c1 - c0) // HALF):
                 fetch(i, k)
-            if i < 2:
-                cast_w2(2 * i)
-                cast_w2(2 * i + 1)
-        quant_w2(0)
-        smaller(last)
 
         dw_g = kt([P, H], U32, "dw_g", tag="hold_d")
-        nc.vector.tensor_copy(dw_g[:], dw_tab[:].indirect(kidx_t[:]))
+        nc.vector.tensor_copy(dw_g[:, :HALF], dw_tab[:].indirect(kidx_t[:, :16]))
+        smaller(last)
+        nc.vector.tensor_copy(dw_g[:, HALF:], dw_tab[:].indirect(kidx_t[:, 16:]))
         quant_z(0)
         dw_d = kt([P, H], U32, "dw_d")
-        nc.vector.tensor_copy(dw_d[:].rearrange("p (t m) -> p m t", t=PACK), dw_g[:].rearrange("p (m t) -> p m t", t=PACK))
+        dealt = dw_d[:].rearrange("p (t m) -> p m t", t=PACK)
+        gathered = dw_g[:].rearrange("p (m t) -> p m t", t=PACK)
+        nc.vector.tensor_copy(dealt[:, :, 0], gathered[:, :, 0])
         quant_z(1)
-        quant_w2(1)
+        nc.vector.tensor_copy(dealt[:, :, 1:], gathered[:, :, 1:])
 
         s = [kt([P, S], F32, f"s{t}") for t in range(PACK)]
         for t in range(PACK):
@@ -196,7 +180,7 @@ def tile_picked_pqkunderduel_none_p_kernel(
                 nc.scalar.activation(s[t][:, cols], acc[:], ACT.Copy, scale=0.0625)
 
         z2_bf = [kt([P, TAIL, PACK], BF16, f"z2_bf{c}") for c in range(S // TAIL)]
-        pair = [kt([P, 2, W], F32, f"pair{t}") for t in range(PACK)]
+        pair = [kt([P, 2, W], F32, f"pair{t}", tag="hold_w2" if t == PACK - 2 else None) for t in range(PACK)]
         odds = [kt([P, 2, W], F32, f"odds{t}") for t in range(PACK)]
         dt = [kt([P, S], F32, f"dt{t}") for t in range(PACK)]
 
@@ -205,8 +189,7 @@ def tile_picked_pqkunderduel_none_p_kernel(
 
         def lead(t):
             diff = ring.tile([P, W], F32, name="diff")
-            eng = nc.vector if t == PACK - 1 else nc.gpsimd
-            eng.tensor_tensor(diff[:], pair[t][:, 0, :], pair[t][:, 1, :], ALU.subtract)
+            nc.vector.tensor_tensor(diff[:], pair[t][:, 0, :], pair[t][:, 1, :], ALU.subtract)
             nc.scalar.activation(odds[t][:, 0, :], diff[:], ACT.Sigmoid)
             nc.scalar.activation(odds[t][:, 1, :], diff[:], ACT.Sigmoid, scale=-1.0)
 
@@ -219,16 +202,29 @@ def tile_picked_pqkunderduel_none_p_kernel(
 
         for t in range(PACK):
             fetch_pair(t, 0)
+            if t >= 1:
+                lead(t - 1)
             fetch_pair(t, 1)
-            if t < PACK - 1:
-                lead(t)
         put(0, 0)
         lead(PACK - 1)
+
+        w2_bf = [kt([P, HALF, PACK], BF16, f"w2_bf{h}", tag=f"s{2 + h}") for h in range(2)]
+        for c in range(PACK):
+            h, c0 = divmod(c * P, HALF)
+            nc.scalar.copy(w2_bf[h][:, c0 : c0 + P, :].rearrange("p (c i) j -> p c j i", i=4),
+                           w2_raw[:, :, c * P : (c + 1) * P].rearrange("p j (c i) -> p c j i", i=4))
+
         for t in range(PACK):
             if t + 1 < PACK:
                 put(t + 1, 0)
             put(t, 1)
             cast_z2(t)
+
+        w2_c = kt([P, N], U32, "w2_c", tag="hold_w2")
+        w2_s = kt([P, N], U8, "w2_s")
+        for h in range(2):
+            cols = slice(h * HALF, (h + 1) * HALF)
+            nc.vector.quantize_mx(w2_c[:, cols].bitcast(FP8X4), w2_s[:, cols], w2_bf[h][:].rearrange("p c j -> p (c j)"))
 
         z2_c = kt([P, S], U32, "z2_c")
         z2_s = kt([P, S], U8, "z2_s")
@@ -238,20 +234,22 @@ def tile_picked_pqkunderduel_none_p_kernel(
         def product(c):
             cols = slice(c * TAIL, (c + 1) * TAIL)
             nc.vector.quantize_mx(z2_c[:, cols].bitcast(FP8X4), z2_s[:, cols], z2_bf[c][:].rearrange("p c t -> p (c t)"))
-            accs[c] = psum.tile([P, PACK, TAIL], F32, name=f"acc_o{c}", tag=f"bank{c}")
-            for t in range(PACK):
-                rows = slice(t % 2 * P, (t % 2 + 1) * P)
-                nc.tensor.matmul_mx(accs[c][:, t, :], lhsT=w2_c[t // 2][:, rows].bitcast(FP8X4), lhsT_scale=w2_s[t // 2][:, rows],
-                                    rhs=z2_c[:, cols].bitcast(FP8X4), rhs_scale=z2_s[:, cols], start=True, stop=True)
+            for u in range(2):
+                accs[c, u] = psum.tile([P, 2, TAIL], F32, name=f"acc_o{c}{u}", tag=f"bank{2 * c + u}")
+                for e in range(2):
+                    rows = slice((2 * u + e) * P, (2 * u + e + 1) * P)
+                    nc.tensor.matmul_mx(accs[c, u][:, e, :], lhsT=w2_c[:, rows].bitcast(FP8X4), lhsT_scale=w2_s[:, rows],
+                                        rhs=z2_c[:, cols].bitcast(FP8X4), rhs_scale=z2_s[:, cols], start=True, stop=True)
 
         def finish(c):
             cols = slice(c * TAIL, (c + 1) * TAIL)
-            total = kt([P, PACK, TAIL], F32, f"total{c}")
-            nc.vector.tensor_tensor(total[:], accs[c][:], res_t[:, :, cols], ALU.add)
-            nc.sync.dma_start(out_rows[:, :, cols], total[:])
+            for u in range(2):
+                total = kt([P, 2, TAIL], F32, f"total{c}{u}")
+                nc.vector.tensor_tensor(total[:], accs[c, u][:], res_t[:, 2 * u : 2 * u + 2, cols], ALU.add)
+                nc.sync.dma_start(out_rows[:, 2 * u : 2 * u + 2, cols], total[:])
 
-        for c in range(S // TAIL + 1):
+        for c in range(S // TAIL + 2):
             if c < S // TAIL:
                 product(c)
-            if c >= 1:
-                finish(c - 1)
+            if c >= 2:
+                finish(c - 2)

from contextlib import ExitStack

import concourse.mybir as mybir

K, T, S, N, H, G, W = 512, 1024, 512, 512, 512, 2048, 256
FLOPS = 3 * 2 * 512 * 512 * 512

F32 = mybir.dt.float32
BF16 = mybir.dt.bfloat16
U32 = mybir.dt.uint32
I32 = mybir.dt.int32
U16 = mybir.dt.uint16
U8 = mybir.dt.uint8
FP8X4 = mybir.dt.float8_e4m3fn_x4
ALU = mybir.AluOpType
ACT = mybir.ActivationFunctionType

P = 128
PACK = 4
HALF = 256
TAIL = 128


def tile_picked_pqkunderduel_none_p_kernel(
    tc, x_words, x_scales, w1, gs, d_words, d_scales, res, gn, w2, offs, n1, n2, kidx, n3, n4, out
):
    nc = tc.nc
    with ExitStack() as ctx:
        lists = ctx.enter_context(tc.tile_pool(name="lists", bufs=1))
        keep = ctx.enter_context(tc.tile_pool(name="keep", bufs=1))
        ring = ctx.enter_context(tc.tile_pool(name="ring", bufs=3))
        psum = ctx.enter_context(tc.psum_pool(name="psum", bufs=1))

        def load_list(src, name):
            dst = lists.tile(list(src.shape), U16, name=name)
            nc.sync.dma_start(dst[:], src)
            return dst

        def kt(shape, dtype, name, tag=None):
            return keep.tile(shape, dtype, name=name, tag=tag or name, align_bytes=64)

        xs_tab = kt([P, T], U8, "xs_tab")
        ds_tab = kt([P, G], U8, "ds_tab")
        ds_fin = kt([P, H], U8, "ds_fin")
        warm = kt([P, 2], F32, "warm")
        nc.gpsimd.memset(xs_tab[:].bitcast(I32), 0)
        nc.gpsimd.memset(warm[:, 0:1], 0.0)
        nc.gpsimd.memset(ds_tab[:].bitcast(I32), 0)
        nc.gpsimd.memset(ds_fin[:].bitcast(I32), 0)

        offs_t = load_list(offs, "offs_t")
        for q in range(4):
            nc.scalar.dma_start(xs_tab[32 * q : 32 * q + 4, :].bitcast(I32), x_scales[0, 4 * q : 4 * q + 4, :].bitcast(I32))
        nc.scalar.activation(warm[:, 1:2], warm[:, 0:1], ACT.Sigmoid)
        xw_tab = kt([P, T], U32, "xw_tab")
        nc.sync.dma_start(xw_tab[:].bitcast(I32), x_words[0].rearrange("p c r -> p (c r)").bitcast(I32))
        w1_rows = w1.rearrange("(p j) c -> p j c", j=PACK)
        w1_raw = []
        for u in range(2):
            raw = kt([P, 2, H], F32, f"w1_raw{u}", tag=f"w1_raw{u}")
            nc.sync.dma_start(raw[:], w1_rows[:, 2 * u : 2 * u + 2, :])
            w1_raw.append(raw)
        kidx_t = load_list(kidx, "kidx_t")
        for q in range(4):
            nc.sync.dma_start(ds_tab[32 * q + 14 : 32 * q + 18, :].bitcast(I32), d_scales[0, 4 * q : 4 * q + 4, :].bitcast(I32))
        n1_t = load_list(n1, "n1_t")
        n2_t = load_list(n2, "n2_t")
        gs_t = kt([P, PACK], F32, "gs_t")
        nc.sync.dma_start(gs_t[:], gs.rearrange("(p t) o -> p (t o)", t=PACK))
        gs_neg = kt([P, PACK], F32, "gs_neg")
        nc.scalar.mul(gs_neg[:], gs_t[:], -1.0)
        dw_tab = kt([P, G], U32, "dw_tab")
        nc.sync.dma_start(dw_tab[:].bitcast(I32), d_words[0].rearrange("p c r -> p (c r)").bitcast(I32))
        n3_t = load_list(n3, "n3_t")
        n4_t = load_list(n4, "n4_t")
        gn_t = kt([P, PACK], F32, "gn_t")
        nc.sync.dma_start(gn_t[:], gn.rearrange("(p t) o -> p (t o)", t=PACK))
        w2_raw = kt([P, PACK, N], F32, "w2_raw")
        nc.sync.dma_start(w2_raw[:], w2.rearrange("(p j) c -> p j c", j=PACK))
        res_t = kt([P, PACK, S], F32, "res_t")
        nc.sync.dma_start(res_t[:], res.rearrange("(t p) j -> p t j", p=P))

        xs = kt([P, S], U8, "xs")
        nc.vector.tensor_copy(xs[:], xs_tab[:].indirect(offs_t[:]))
        xw = kt([P, S], U32, "xw")
        nc.vector.tensor_copy(xw[:], xw_tab[:].indirect(offs_t[:]))

        w1_bf = [kt([P, 2, P, PACK], BF16, f"w1_bf{v}") for v in range(2)]
        for u in range(2):
            for v in range(2):
                copy = nc.vector.tensor_copy if (u, v) == (1, 0) else nc.scalar.copy
                dst = w1_bf[v][:, :, :, 2 * u : 2 * u + 2].rearrange("p t m j -> p m j t")
                src = w1_raw[u][:].rearrange("p j (m t) -> p m j t", t=PACK)[:, :, :, 2 * v : 2 * v + 2]
                copy(dst, src)

        w1_c = kt([P, H], U32, "w1_c")
        w1_s = kt([P, H], U8, "w1_s")
        y, y_again = [], []
        for t in range(PACK):
            cols = slice(t * P, (t + 1) * P)
            nc.vector.quantize_mx(w1_c[:, cols].bitcast(FP8X4), w1_s[:, cols], w1_bf[t // 2][:, t % 2].rearrange("p m j -> p (m j)"))
            acc = psum.tile([P, S], F32, name=f"acc_y{t}", tag=f"bank{t}")
            nc.tensor.matmul_mx(acc[:], lhsT=w1_c[:, cols].bitcast(FP8X4), lhsT_scale=w1_s[:, cols],
                                rhs=xw[:].bitcast(FP8X4), rhs_scale=xs[:], start=True, stop=True)
            y_t = kt([P, S], F32, f"y{t}")
            twin = kt([P, S], F32, f"y_again{t}")
            nc.scalar.copy(twin[:, :HALF], acc[:, :HALF])
            nc.scalar.copy(y_t[:], acc[:])
            nc.scalar.copy(twin[:, HALF:], acc[:, HALF:])
            y.append(y_t)
            y_again.append(twin)

        ds_g = kt([P, H], U8, "ds_g", tag="w1_raw1")
        nc.vector.tensor_copy(ds_g[:], ds_tab[:].indirect(kidx_t[:]))
        ds_d = kt([P, H], U8, "ds_d")
        nc.vector.tensor_copy(ds_d[:].rearrange("p (t m) -> p m t", t=PACK), ds_g[:].rearrange("p (m t) -> p m t", t=PACK))
        for q in range(4):
            nc.sync.dma_start(ds_fin[32 * q : 32 * q + 4, :].bitcast(I32), ds_d[32 * q + 14 : 32 * q + 18, :].bitcast(I32))

        z_bf = [kt([P, HALF, PACK], BF16, f"z_bf{h}", tag=f"z_bf{h}") for h in range(2)]
        steps = [(t, 0, S) for t in range(PACK - 1)] + [(PACK - 1, 0, HALF), (PACK - 1, HALF, S)]
        last = len(steps) - 1
        picked = {}

        def fetch(i, k):
            t, c0, c1 = steps[i]
            if k == 0:
                if i == last - 1:
                    picked[i] = kt([P, 2, c1 - c0], F32, "picked_late", tag="hold_d")
                else:
                    picked[i] = ring.tile([P, 2, c1 - c0], F32, name="picked")
            which, off = k % 2, (k // 2) * HALF
            lst = (n1_t, n2_t)[which]
            nc.vector.tensor_tensor(picked[i][:, which, off : off + HALF],
                                    y[t][:].indirect(lst[:, (c0 + off) // 16 : (c0 + off + HALF) // 16]),
                                    y_again[t][:, c0 + off : c0 + off + HALF], ALU.subtract)

        def smaller(i):
            t, c0, c1 = steps[i]
            least = ring.tile([P, c1 - c0], F32, name="least")
            nc.vector.tensor_tensor(least[:], picked[i][:, 0, :], picked[i][:, 1, :], ALU.min)
            for c in range(c0, c1, HALF):
                nc.scalar.activation(z_bf[c // HALF][:, :, t], least[:, c - c0 : c - c0 + HALF], ACT.Copy, scale=gs_neg[:, t : t + 1])

        z_c = kt([P, S], U32, "z_c")
        z_s = kt([P, S], U8, "z_s")

        def quant_z(h):
            cols = slice(h * HALF, (h + 1) * HALF)
            nc.vector.quantize_mx(z_c[:, cols].bitcast(FP8X4), z_s[:, cols], z_bf[h][:].rearrange("p c t -> p (c t)"))

        for i in range(last + 1):
            t, c0, c1 = steps[i]
            fetch(i, 0)
            if i >= 1:
                smaller(i - 1)
            for k in range(1, 2 * (c1 - c0) // HALF):
                fetch(i, k)

        dw_g = kt([P, H], U32, "dw_g", tag="hold_d")
        nc.vector.tensor_copy(dw_g[:, :HALF], dw_tab[:].indirect(kidx_t[:, :16]))
        smaller(last)
        nc.vector.tensor_copy(dw_g[:, HALF:], dw_tab[:].indirect(kidx_t[:, 16:]))
        quant_z(0)
        dw_d = kt([P, H], U32, "dw_d")
        dealt = dw_d[:].rearrange("p (t m) -> p m t", t=PACK)
        gathered = dw_g[:].rearrange("p (m t) -> p m t", t=PACK)
        nc.vector.tensor_copy(dealt[:, :, 0], gathered[:, :, 0])
        quant_z(1)
        nc.vector.tensor_copy(dealt[:, :, 1:], gathered[:, :, 1:])

        s = [kt([P, S], F32, f"s{t}") for t in range(PACK)]
        for t in range(PACK):
            keys = slice(t * P, (t + 1) * P)
            for h in range(2):
                cols = slice(h * HALF, (h + 1) * HALF)
                acc = psum.tile([P, HALF], F32, name=f"acc_s{t}{h}", tag=f"bank{4 * (1 - h) + t}")
                nc.tensor.matmul_mx(acc[:], lhsT=dw_d[:, keys].bitcast(FP8X4), lhsT_scale=ds_fin[:, keys],
                                    rhs=z_c[:, cols].bitcast(FP8X4), rhs_scale=z_s[:, cols], start=True, stop=True)
                nc.scalar.activation(s[t][:, cols], acc[:], ACT.Copy, scale=0.0625)

        z2_bf = [kt([P, TAIL, PACK], BF16, f"z2_bf{c}") for c in range(S // TAIL)]
        pair = [kt([P, 2, W], F32, f"pair{t}", tag="hold_w2" if t == PACK - 2 else None) for t in range(PACK)]
        odds = [kt([P, 2, W], F32, f"odds{t}") for t in range(PACK)]
        dt = [kt([P, S], F32, f"dt{t}") for t in range(PACK)]

        def fetch_pair(t, which):
            nc.vector.tensor_copy(pair[t][:, which, :], s[t][:].indirect((n3_t, n4_t)[which][:]))

        def lead(t):
            diff = ring.tile([P, W], F32, name="diff")
            nc.vector.tensor_tensor(diff[:], pair[t][:, 0, :], pair[t][:, 1, :], ALU.subtract)
            nc.scalar.activation(odds[t][:, 0, :], diff[:], ACT.Sigmoid)
            nc.scalar.activation(odds[t][:, 1, :], diff[:], ACT.Sigmoid, scale=-1.0)

        def put(t, which):
            nc.vector.tensor_tensor(dt[t][:].indirect((n3_t, n4_t)[which][:]), pair[t][:, which, :], odds[t][:, which, :], ALU.mult)

        def cast_z2(t):
            for c in range(S // TAIL):
                nc.scalar.activation(z2_bf[c][:, :, t], dt[t][:, c * TAIL : (c + 1) * TAIL], ACT.Copy, scale=gn_t[:, t : t + 1])

        for t in range(PACK):
            fetch_pair(t, 0)
            if t >= 1:
                lead(t - 1)
            fetch_pair(t, 1)
        put(0, 0)
        lead(PACK - 1)

        w2_bf = [kt([P, HALF, PACK], BF16, f"w2_bf{h}", tag=f"s{2 + h}") for h in range(2)]
        for c in range(PACK):
            h, c0 = divmod(c * P, HALF)
            nc.scalar.copy(w2_bf[h][:, c0 : c0 + P, :].rearrange("p (c i) j -> p c j i", i=4),
                           w2_raw[:, :, c * P : (c + 1) * P].rearrange("p j (c i) -> p c j i", i=4))

        for t in range(PACK):
            if t + 1 < PACK:
                put(t + 1, 0)
            put(t, 1)
            cast_z2(t)

        w2_c = kt([P, N], U32, "w2_c", tag="hold_w2")
        w2_s = kt([P, N], U8, "w2_s")
        for h in range(2):
            cols = slice(h * HALF, (h + 1) * HALF)
            nc.vector.quantize_mx(w2_c[:, cols].bitcast(FP8X4), w2_s[:, cols], w2_bf[h][:].rearrange("p c j -> p (c j)"))

        z2_c = kt([P, S], U32, "z2_c")
        z2_s = kt([P, S], U8, "z2_s")
        out_rows = out.rearrange("(t p) j -> p t j", p=P)
        accs = {}

        def product(c):
            cols = slice(c * TAIL, (c + 1) * TAIL)
            nc.vector.quantize_mx(z2_c[:, cols].bitcast(FP8X4), z2_s[:, cols], z2_bf[c][:].rearrange("p c t -> p (c t)"))
            for u in range(2):
                accs[c, u] = psum.tile([P, 2, TAIL], F32, name=f"acc_o{c}{u}", tag=f"bank{2 * c + u}")
                for e in range(2):
                    rows = slice((2 * u + e) * P, (2 * u + e + 1) * P)
                    nc.tensor.matmul_mx(accs[c, u][:, e, :], lhsT=w2_c[:, rows].bitcast(FP8X4), lhsT_scale=w2_s[:, rows],
                                        rhs=z2_c[:, cols].bitcast(FP8X4), rhs_scale=z2_s[:, cols], start=True, stop=True)

        def finish(c):
            cols = slice(c * TAIL, (c + 1) * TAIL)
            for u in range(2):
                total = kt([P, 2, TAIL], F32, f"total{c}{u}")
                nc.vector.tensor_tensor(total[:], accs[c, u][:], res_t[:, 2 * u : 2 * u + 2, cols], ALU.add)
                nc.sync.dma_start(out_rows[:, 2 * u : 2 * u + 2, cols], total[:])

        for c in range(S // TAIL + 2):
            if c < S // TAIL:
                product(c)
            if c >= 2:
                finish(c - 2)
